import numpy as np
import ml_dtypes


def mxq(x, axis, fmt="e4m3"):
    dtype, down = {"e4m3": (ml_dtypes.float8_e4m3fn, 7), "e5m2": (ml_dtypes.float8_e5m2, 14)}[fmt]
    v = np.moveaxis(np.asarray(x, np.float32).astype(ml_dtypes.bfloat16).astype(np.float64), axis, -1)
    blocks = v.reshape(v.shape[:-1] + (-1, 32))
    amax = np.abs(blocks).max(-1, keepdims=True)
    byte = np.maximum(np.where(amax > 0, np.frexp(amax)[1] - 1 + 127, 0) - down, 1)
    scale = np.exp2(byte - 127.0)
    codes = (blocks / scale).astype(np.float32).astype(dtype).astype(np.float64)
    return np.moveaxis((codes * scale).reshape(v.shape), -1, axis)


WIDE = False


def mx_kscale(k):
    if not WIDE:
        return np.ones(k)
    levels = np.array([10, -10, 5, -5, 0])
    if k % 512:
        return np.exp2(np.random.permutation(np.resize(levels, k // 32))).repeat(32)
    a = np.empty((k // 512, 16))
    for p in range(k // 512):
        a[p, :8] = np.random.permutation(np.resize(levels, 8))
        for g in range(8):
            far = levels[np.abs(levels - a[p, g]) >= 10]
            a[p, g + 8] = far[np.random.randint(len(far))]
    return np.exp2(a.ravel()).repeat(32)


def f64(x):
    return np.asarray(x).astype(np.float64)


def striped(idx):
    return np.tile(idx.reshape(-1, 16).T, (8, 1)).astype(np.uint16)


def unstriped(offs):
    return offs[:16].T.reshape(-1).astype(np.int64)


E2M1 = np.array([0.0, 0.5, 1.0, 1.5, 2.0, 3.0, 4.0, 6.0, -0.0, -0.5, -1.0, -1.5, -2.0, -3.0, -4.0, -6.0])


def pack_weight(w, fmt):
    k, n = w.shape
    w = f64(np.asarray(w, np.float32).astype(ml_dtypes.bfloat16)).reshape(k // 32, 32, n)
    amax = np.abs(w).max(1)
    if fmt == "e4m3":
        byte = np.frexp(amax)[1] - 1 + 127 - 7
    else:
        mant, ex = np.frexp(amax / 6.0)
        byte = np.where(mant > 0.5, ex, ex - 1) + 127
    byte = np.clip(np.where(amax > 0, byte, 1), 1, 254)
    scaled = (w * np.exp2(127.0 - byte)[:, None, :]).reshape(k, n).astype(np.float32)
    by_word = np.ascontiguousarray(scaled.reshape(k // 512, 128, 4, n).transpose(0, 1, 3, 2))
    if fmt == "e4m3":
        words = by_word.astype(ml_dtypes.float8_e4m3fn).view(np.uint8)
    else:
        c = by_word.astype(ml_dtypes.float4_e2m1fn).view(np.uint8) & 0xF
        words = (c[..., 0::2] | (c[..., 1::2] << 4)).reshape(k // 512, 128, 2 * n)
    return np.ascontiguousarray(words), np.ascontiguousarray(byte.astype(np.uint8).reshape(k // 512, 16, n))


def unpack_weight(words, scales, fmt):
    g, _, n = scales.shape
    words = np.ascontiguousarray(words).reshape(g, 128, n, -1)
    if fmt == "e4m3":
        vals = words.view(ml_dtypes.float8_e4m3fn).astype(np.float64)
    else:
        nib = np.empty((g, 128, n, 4), np.uint8)
        nib[..., 0::2] = words & 0xF
        nib[..., 1::2] = words >> 4
        vals = E2M1[nib]
    vals = vals * np.repeat(np.exp2(scales.astype(np.float64) - 127.0), 8, axis=1)[..., None]
    return vals.transpose(0, 1, 3, 2).reshape(g * 512, n)


def silu(v):
    return v / (1.0 + np.exp(-np.maximum(v, -700.0)))


K, T, E, C, N = 2048, 2048, 6, 128, 512


def by_slot(wq, xq):
    return np.concatenate([xq[:, e * C:(e + 1) * C].T @ wq[e] for e in range(E)])


def setup_inputs():
    n = np.random.standard_normal
    s = mx_kscale(K)
    slot_token = np.concatenate([np.random.permutation(T)[:C] for e in range(E)])
    x = pack_weight(n((K, T)) * s[:, None], "e2m1")
    two = np.ascontiguousarray(x[0].reshape(K // 1024, 2, 128, T, 2).transpose(0, 2, 3, 1, 4).reshape(K // 1024, 128, T, 4))
    return {
        "x_words": two,
        "x_scales": x[1],
        "w": (n((E, K, N)) / np.sqrt(K) / s[None, :, None]).astype(np.float32),
        "offs": striped(slot_token),
    }


def reference(x_words, x_scales, w, offs):
    wq = mxq(f64(w), 1, "e4m3")
    idx = unstriped(offs)
    words = x_words.reshape(K // 1024, 128, T, 2, 2).transpose(0, 3, 1, 2, 4).reshape(K // 512, 128, 2 * T)
    xq = unpack_weight(words, x_scales, "e2m1")[:, idx]
    y = silu(by_slot(wq, xq))
    return y

@@ -1,0 +1,110 @@
+from contextlib import ExitStack
+
+import concourse.mybir as mybir
+
+K, T, E, C, N = 2048, 2048, 6, 128, 512
+P = 128
+PACK = 4
+K_PASS = P * PACK
+PASSES = K // K_PASS
+SLOTS = E * C
+RAW_SLOTS = 10
+FLOPS = 2 * SLOTS * K * N
+
+F32 = mybir.dt.float32
+BF16 = mybir.dt.bfloat16
+I32 = mybir.dt.int32
+U32 = mybir.dt.uint32
+U16 = mybir.dt.uint16
+U8 = mybir.dt.uint8
+FP8X4 = mybir.dt.float8_e4m3fn_x4
+FP4X4 = mybir.dt.float4_e2m1fn_x4
+SILU = mybir.ActivationFunctionType.Silu
+
+
+def tile_moe_s_lin_silu_kernel(tc, x_words, x_scales, w, offs, out):
+    nc = tc.nc
+    with ExitStack() as ctx:
+        keep = ctx.enter_context(tc.tile_pool(name="keep", bufs=1))
+        stage = ctx.enter_context(tc.tile_pool(name="stage", bufs=3))
+        psum = ctx.enter_context(tc.psum_pool(name="psum", bufs=1))
+
+        scale_table = keep.tile([P, T], U8, name="scale_table", align_bytes=64)
+        planes = keep.tile([P, PASSES * SLOTS], U8, name="planes", align_bytes=64)
+        nc.vector.memset(scale_table[:].bitcast(I32), 0)
+        nc.vector.memset(planes[:].bitcast(I32), 0)
+
+        offsets = keep.tile([P, SLOTS // 16], U16, name="offsets")
+        word_tables = []
+        for m in range(PASSES // 2):
+            table = keep.tile([P, T], I32, name="word_table%d" % m, align_bytes=64)
+            nc.sync.dma_start(out=table[:], in_=x_words[m].rearrange("p t d -> p (t d)").bitcast(I32))
+            word_tables.append(table)
+            if m == 0:
+                nc.sync.dma_start(offsets[:], offs)
+                nc.sync.dma_start(
+                    out=scale_table[0:P:2, :].bitcast(I32),
+                    in_=x_scales.bitcast(I32).rearrange("s b t -> b s t"),
+                )
+
+        slot_scales = keep.tile([P, SLOTS], U8, name="slot_scales", align_bytes=64)
+        nc.vector.tensor_copy(slot_scales[:], scale_table[:].indirect(offsets[:]))
+        for q in range(4):
+            nc.sync.dma_start(
+                out=planes[32 * q : 32 * q + 4, :].bitcast(I32),
+                in_=slot_scales[32 * q : 32 * q + 32 : 2, :].bitcast(I32),
+            )
+
+        tokens = []
+        for m in range(PASSES // 2):
+            pairs = keep.tile([P, SLOTS], U32, name="pairs%d" % m, align_bytes=64)
+            nc.vector.tensor_copy(pairs[:], word_tables[m][:].bitcast(U32).indirect(offsets[:]))
+            parted = keep.tile([P, 2 * 2 * SLOTS], U8, name="parted%d" % m, align_bytes=64)
+            nc.vector.tensor_copy(
+                out=parted[:].bitcast(U16).rearrange("p (q j) -> p q j", q=2),
+                in_=pairs[:].bitcast(U16).rearrange("p (j q) -> p q j", q=2),
+            )
+            tokens.append(parted)
+
+        sums = [psum.tile([P, N], F32, name="sums%d" % e) for e in range(E)]
+        chunks = E * PASSES
+        half = N // 2
+        for c in range(chunks):
+            e, s = divmod(c, PASSES)
+            raw = keep.tile([P, PACK, N], F32, name="raw", tag="slot%d" % (c % RAW_SLOTS))
+            nc.sync.dma_start(
+                out=raw[:],
+                in_=w[e, s * K_PASS : (s + 1) * K_PASS, :].rearrange("(p j) n -> p j n", j=PACK),
+            )
+            grouped = stage.tile([P, N, PACK], BF16, name="grouped", align_bytes=64)
+            nc.scalar.copy(
+                out=grouped[:, half:, :].rearrange("p (c i) j -> p c j i", i=4),
+                in_=raw[:, :, half:].rearrange("p j (c i) -> p c j i", i=4),
+            )
+            nc.vector.tensor_copy(
+                out=grouped[:, :half, :].rearrange("p (c i) j -> p c j i", i=4),
+                in_=raw[:, :, :half].rearrange("p j (c i) -> p c j i", i=4),
+            )
+            codes = keep.tile([P, N], U32, name="codes%d" % c, align_bytes=64)
+            scales = keep.tile([P, N], U8, name="scales%d" % c, align_bytes=64)
+            nc.vector.quantize_mx(
+                out=codes[:].bitcast(FP8X4),
+                scales=scales[:],
+                in_=grouped[:].rearrange("p n j -> p (n j)"),
+            )
+            first = (s % 2) * SLOTS + e * C
+            nc.tensor.matmul_mx(
+                out=sums[e][:],
+                lhsT=tokens[s // 2][:, 2 * first : 2 * (first + C)].bitcast(FP4X4),
+                lhsT_scale=planes[:, s * SLOTS + e * C : s * SLOTS + (e + 1) * C],
+                rhs=codes[:].bitcast(FP8X4),
+                rhs_scale=scales[:],
+                start=(s == 0),
+                stop=(s == PASSES - 1),
+            )
+
+        for e in range(E):
+            slot = (chunks - RAW_SLOTS + e) % RAW_SLOTS
+            result = keep.tile([P, N], F32, name="result", tag="slot%d" % slot)
+            nc.scalar.activation(result[:], sums[e][:], SILU)
+            nc.sync.dma_start(out=out[e * C : (e + 1) * C, :], in_=result[:])

@@ -8,7 +8,7 @@ PACK = 4
 K_PASS = P * PACK
 PASSES = K // K_PASS
 SLOTS = E * C
-RAW_SLOTS = 10
+RAW_SLOTS = 3
 FLOPS = 2 * SLOTS * K * N
 
 F32 = mybir.dt.float32
@@ -35,17 +35,13 @@ def tile_moe_s_lin_silu_kernel(tc, x_words, x_scales, w, offs, out):
         nc.vector.memset(planes[:].bitcast(I32), 0)
 
         offsets = keep.tile([P, SLOTS // 16], U16, name="offsets")
-        word_tables = []
-        for m in range(PASSES // 2):
-            table = keep.tile([P, T], I32, name="word_table%d" % m, align_bytes=64)
-            nc.sync.dma_start(out=table[:], in_=x_words[m].rearrange("p t d -> p (t d)").bitcast(I32))
-            word_tables.append(table)
-            if m == 0:
-                nc.sync.dma_start(offsets[:], offs)
-                nc.sync.dma_start(
-                    out=scale_table[0:P:2, :].bitcast(I32),
-                    in_=x_scales.bitcast(I32).rearrange("s b t -> b s t"),
-                )
+        word_table = keep.tile([P, PASSES // 2, T], I32, name="word_table", align_bytes=64)
+        nc.sync.dma_start(out=word_table[:], in_=x_words.rearrange("m p t d -> p m (t d)").bitcast(I32))
+        nc.sync.dma_start(offsets[:], offs)
+        nc.sync.dma_start(
+            out=scale_table[0:P:2, :].bitcast(I32),
+            in_=x_scales.bitcast(I32).rearrange("s b t -> b s t"),
+        )
 
         slot_scales = keep.tile([P, SLOTS], U8, name="slot_scales", align_bytes=64)
         nc.vector.tensor_copy(slot_scales[:], scale_table[:].indirect(offsets[:]))
@@ -58,7 +54,7 @@ def tile_moe_s_lin_silu_kernel(tc, x_words, x_scales, w, offs, out):
         tokens = []
         for m in range(PASSES // 2):
             pairs = keep.tile([P, SLOTS], U32, name="pairs%d" % m, align_bytes=64)
-            nc.vector.tensor_copy(pairs[:], word_tables[m][:].bitcast(U32).indirect(offsets[:]))
+            nc.vector.tensor_copy(pairs[:], word_table[:, m, :].bitcast(U32).indirect(offsets[:]))
             parted = keep.tile([P, 2 * 2 * SLOTS], U8, name="parted%d" % m, align_bytes=64)
             nc.vector.tensor_copy(
                 out=parted[:].bitcast(U16).rearrange("p (q j) -> p q j", q=2),
@@ -66,45 +62,88 @@ def tile_moe_s_lin_silu_kernel(tc, x_words, x_scales, w, offs, out):
             )
             tokens.append(parted)
 
-        sums = [psum.tile([P, N], F32, name="sums%d" % e) for e in range(E)]
-        chunks = E * PASSES
-        half = N // 2
-        for c in range(chunks):
-            e, s = divmod(c, PASSES)
-            raw = keep.tile([P, PACK, N], F32, name="raw", tag="slot%d" % (c % RAW_SLOTS))
+        def load(raw, e, s0, s1):
             nc.sync.dma_start(
-                out=raw[:],
-                in_=w[e, s * K_PASS : (s + 1) * K_PASS, :].rearrange("(p j) n -> p j n", j=PACK),
+                out=raw[:, s0:s1],
+                in_=w[e, s0 * K_PASS : s1 * K_PASS, :].rearrange("(s p j) n -> p s j n", p=P, j=PACK),
             )
-            grouped = stage.tile([P, N, PACK], BF16, name="grouped", align_bytes=64)
-            nc.scalar.copy(
-                out=grouped[:, half:, :].rearrange("p (c i) j -> p c j i", i=4),
-                in_=raw[:, :, half:].rearrange("p j (c i) -> p c j i", i=4),
+
+        def group(copy, grouped, rows, cols):
+            copy(
+                out=grouped[:, cols, :].rearrange("p (c i) j -> p c j i", i=4),
+                in_=rows[:, :, cols].rearrange("p j (c i) -> p c j i", i=4),
             )
-            nc.vector.tensor_copy(
-                out=grouped[:, :half, :].rearrange("p (c i) j -> p c j i", i=4),
-                in_=raw[:, :, :half].rearrange("p j (c i) -> p c j i", i=4),
-            )
-            codes = keep.tile([P, N], U32, name="codes%d" % c, align_bytes=64)
-            scales = keep.tile([P, N], U8, name="scales%d" % c, align_bytes=64)
+
+        def quantise(codes, scales, grouped, cols):
             nc.vector.quantize_mx(
-                out=codes[:].bitcast(FP8X4),
-                scales=scales[:],
-                in_=grouped[:].rearrange("p n j -> p (n j)"),
+                out=codes[:, cols].bitcast(FP8X4),
+                scales=scales[:, cols],
+                in_=grouped[:, cols, :].rearrange("p n j -> p (n j)"),
             )
+
+        def multiply(acc, e, s, codes, scales, cols):
             first = (s % 2) * SLOTS + e * C
             nc.tensor.matmul_mx(
-                out=sums[e][:],
+                out=acc,
                 lhsT=tokens[s // 2][:, 2 * first : 2 * (first + C)].bitcast(FP4X4),
                 lhsT_scale=planes[:, s * SLOTS + e * C : s * SLOTS + (e + 1) * C],
-                rhs=codes[:].bitcast(FP8X4),
-                rhs_scale=scales[:],
+                rhs=codes[:, cols].bitcast(FP8X4),
+                rhs_scale=scales[:, cols],
                 start=(s == 0),
                 stop=(s == PASSES - 1),
             )
 
-        for e in range(E):
-            slot = (chunks - RAW_SLOTS + e) % RAW_SLOTS
-            result = keep.tile([P, N], F32, name="result", tag="slot%d" % slot)
-            nc.scalar.activation(result[:], sums[e][:], SILU)
-            nc.sync.dma_start(out=out[e * C : (e + 1) * C, :], in_=result[:])
+        last = E - 1
+        half = N // 2
+        blocks = [slice(b * P, (b + 1) * P) for b in range(N // P)]
+        sums = []
+        for e in range(last):
+            raw = keep.tile([P, PASSES, PACK, N], F32, name="raw", tag="slot%d" % (e % RAW_SLOTS))
+            load(raw, e, 0, PASSES)
+            acc = psum.tile([P, N], F32, name="acc", tag="bank%d" % e)
+            sums.append(acc)
+            for s in range(PASSES):
+                grouped = stage.tile([P, N, PACK], BF16, name="grouped", align_bytes=64)
+                group(nc.scalar.copy, grouped, raw[:, s], slice(half, N))
+                group(nc.vector.tensor_copy, grouped, raw[:, s], slice(0, half))
+                codes = keep.tile([P, N], U32, name="codes%d_%d" % (e, s), align_bytes=64)
+                scales = keep.tile([P, N], U8, name="scales%d_%d" % (e, s), align_bytes=64)
+                quantise(codes, scales, grouped, slice(0, N))
+                multiply(acc[:], e, s, codes, scales, slice(0, N))
+
+        raw = keep.tile([P, PASSES, PACK, N], F32, name="raw", tag="slot%d" % (last % RAW_SLOTS))
+        load(raw, last, 0, 2)
+        load(raw, last, 2, 3)
+        load(raw, last, 3, 4)
+
+        early = keep.tile([P, last - 1, N], F32, name="early", tag="slot%d" % ((last - 2) % RAW_SLOTS))
+        for e in range(last - 1):
+            nc.scalar.activation(early[:, e, :], sums[e][:], SILU)
+        nc.sync.dma_start(out=out[: (last - 1) * C, :].rearrange("(e p) n -> p e n", p=P), in_=early[:])
+        result = keep.tile([P, N], F32, name="result")
+        nc.scalar.activation(result[:], sums[last - 1][:], SILU)
+        nc.sync.dma_start(out=out[(last - 1) * C : last * C, :], in_=result[:])
+
+        accs = [psum.tile([P, P], F32, name="acc", tag="bank%d" % ((last + b) % 8)) for b in range(len(blocks))]
+        final = keep.tile([P, N], F32, name="final")
+        for s in range(PASSES):
+            grouped = stage.tile([P, N, PACK], BF16, name="grouped", align_bytes=64)
+            codes = keep.tile([P, N], U32, name="codes%d_%d" % (last, s), align_bytes=64)
+            scales = keep.tile([P, N], U8, name="scales%d_%d" % (last, s), align_bytes=64)
+            if s < PASSES - 1:
+                group(nc.scalar.copy, grouped, raw[:, s], slice(half, N))
+                group(nc.vector.tensor_copy, grouped, raw[:, s], slice(0, half))
+                quantise(codes, scales, grouped, slice(0, N))
+                for b, cols in enumerate(blocks):
+                    multiply(accs[b][:], last, s, codes, scales, cols)
+            else:
+                for b, cols in enumerate(blocks):
+                    group(nc.vector.tensor_copy if b < 2 else nc.scalar.copy, grouped, raw[:, s], cols)
+                for b, cols in enumerate(blocks):
+                    quantise(codes, scales, grouped, cols)
+                    multiply(accs[b][:], last, s, codes, scales, cols)
+        for b, cols in enumerate(blocks):
+            nc.scalar.activation(final[:, cols], accs[b][:], SILU)
+            if b % 2 == 1:
+                both = slice((b - 1) * P, (b + 1) * P)
+                nc.sync.dma_start(out=out[last * C :, both], in_=final[:, both])

@@ -70,8 +70,8 @@ def tile_moe_s_lin_silu_kernel(tc, x_words, x_scales, w, offs, out):
 
         def group(copy, grouped, rows, cols):
             copy(
-                out=grouped[:, cols, :].rearrange("p (c i) j -> p c j i", i=4),
-                in_=rows[:, :, cols].rearrange("p j (c i) -> p c j i", i=4),
+                out=grouped[:, cols, :].rearrange("p (c i) j -> p c j i", i=2),
+                in_=rows[:, :, cols].rearrange("p j (c i) -> p c j i", i=2),
             )
 
         def quantise(codes, scales, grouped, cols):
@@ -99,7 +99,9 @@ def tile_moe_s_lin_silu_kernel(tc, x_words, x_scales, w, offs, out):
         sums = []
         for e in range(last):
             raw = keep.tile([P, PASSES, PACK, N], F32, name="raw", tag="slot%d" % (e % RAW_SLOTS))
-            load(raw, e, 0, PASSES)
+            step = PASSES if e < last - 1 else PASSES // 2
+            for s0 in range(0, PASSES, step):
+                load(raw, e, s0, s0 + step)
             acc = psum.tile([P, N], F32, name="acc", tag="bank%d" % e)
             sums.append(acc)
             for s in range(PASSES):
@@ -112,9 +114,8 @@ def tile_moe_s_lin_silu_kernel(tc, x_words, x_scales, w, offs, out):
                 multiply(acc[:], e, s, codes, scales, slice(0, N))
 
         raw = keep.tile([P, PASSES, PACK, N], F32, name="raw", tag="slot%d" % (last % RAW_SLOTS))
-        load(raw, last, 0, 2)
-        load(raw, last, 2, 3)
-        load(raw, last, 3, 4)
+        for s in range(PASSES):
+            load(raw, last, s, s + 1)
 
         early = keep.tile([P, last - 1, N], F32, name="early", tag="slot%d" % ((last - 2) % RAW_SLOTS))
         for e in range(last - 1):

@@ -8,7 +8,7 @@ PACK = 4
 K_PASS = P * PACK
 PASSES = K // K_PASS
 SLOTS = E * C
-RAW_SLOTS = 3
+RAW_SLOTS = 10
 FLOPS = 2 * SLOTS * K * N
 
 F32 = mybir.dt.float32
@@ -26,7 +26,6 @@ def tile_moe_s_lin_silu_kernel(tc, x_words, x_scales, w, offs, out):
     nc = tc.nc
     with ExitStack() as ctx:
         keep = ctx.enter_context(tc.tile_pool(name="keep", bufs=1))
-        stage = ctx.enter_context(tc.tile_pool(name="stage", bufs=3))
         psum = ctx.enter_context(tc.psum_pool(name="psum", bufs=1))
 
         scale_table = keep.tile([P, T], U8, name="scale_table", align_bytes=64)
@@ -35,18 +34,22 @@ def tile_moe_s_lin_silu_kernel(tc, x_words, x_scales, w, offs, out):
         nc.vector.memset(planes[:].bitcast(I32), 0)
 
         offsets = keep.tile([P, SLOTS // 16], U16, name="offsets")
-        word_table = keep.tile([P, PASSES // 2, T], I32, name="word_table", align_bytes=64)
-        nc.sync.dma_start(out=word_table[:], in_=x_words.rearrange("m p t d -> p m (t d)").bitcast(I32))
-        nc.sync.dma_start(offsets[:], offs)
-        nc.sync.dma_start(
-            out=scale_table[0:P:2, :].bitcast(I32),
-            in_=x_scales.bitcast(I32).rearrange("s b t -> b s t"),
-        )
+        word_tables = []
+        for m in range(PASSES // 2):
+            table = keep.tile([P, T], I32, name="word_table%d" % m, align_bytes=64)
+            nc.sync.dma_start(out=table[:], in_=x_words[m].rearrange("p t d -> p (t d)").bitcast(I32))
+            word_tables.append(table)
+            if m == 0:
+                nc.sync.dma_start(offsets[:], offs)
+                nc.sync.dma_start(
+                    out=scale_table[0:P:2, :].bitcast(I32),
+                    in_=x_scales.bitcast(I32).rearrange("s b t -> b s t"),
+                )
 
         slot_scales = keep.tile([P, SLOTS], U8, name="slot_scales", align_bytes=64)
         nc.vector.tensor_copy(slot_scales[:], scale_table[:].indirect(offsets[:]))
         for q in range(4):
-            nc.sync.dma_start(
+            nc.scalar.dma_start(
                 out=planes[32 * q : 32 * q + 4, :].bitcast(I32),
                 in_=slot_scales[32 * q : 32 * q + 32 : 2, :].bitcast(I32),
             )
@@ -54,7 +57,7 @@ def tile_moe_s_lin_silu_kernel(tc, x_words, x_scales, w, offs, out):
         tokens = []
         for m in range(PASSES // 2):
             pairs = keep.tile([P, SLOTS], U32, name="pairs%d" % m, align_bytes=64)
-            nc.vector.tensor_copy(pairs[:], word_table[:, m, :].bitcast(U32).indirect(offsets[:]))
+            nc.vector.tensor_copy(pairs[:], word_tables[m][:].bitcast(U32).indirect(offsets[:]))
             parted = keep.tile([P, 2 * 2 * SLOTS], U8, name="parted%d" % m, align_bytes=64)
             nc.vector.tensor_copy(
                 out=parted[:].bitcast(U16).rearrange("p (q j) -> p q j", q=2),
@@ -62,23 +65,29 @@ def tile_moe_s_lin_silu_kernel(tc, x_words, x_scales, w, offs, out):
             )
             tokens.append(parted)
 
-        def load(raw, e, s0, s1):
-            nc.sync.dma_start(
-                out=raw[:, s0:s1],
-                in_=w[e, s0 * K_PASS : s1 * K_PASS, :].rearrange("(s p j) n -> p s j n", p=P, j=PACK),
-            )
+        last = E - 1
+        half = N // 2
 
-        def group(copy, grouped, rows, cols):
+        def rows_of(e, s):
+            return w[e, s * K_PASS : (s + 1) * K_PASS, :].rearrange("(p j) n -> p j n", j=PACK)
+
+        def slot(e, s):
+            return "slot%d" % ((e * PASSES + s) % RAW_SLOTS)
+
+        def load(e, s):
+            raw = keep.tile([P, PACK, N], F32, name="raw", tag=slot(e, s))
+            nc.sync.dma_start(out=raw[:], in_=rows_of(e, s))
+            return [raw[:, :, :half], raw[:, :, half:]]
+
+        def group(copy, grouped, rows):
             copy(
-                out=grouped[:, cols, :].rearrange("p (c i) j -> p c j i", i=2),
-                in_=rows[:, :, cols].rearrange("p j (c i) -> p c j i", i=2),
+                out=grouped.rearrange("p (c i) j -> p c j i", i=2),
+                in_=rows.rearrange("p j (c i) -> p c j i", i=2),
             )
 
-        def quantise(codes, scales, grouped, cols):
+        def quantise(codes, scales, grouped):
             nc.vector.quantize_mx(
-                out=codes[:, cols].bitcast(FP8X4),
-                scales=scales[:, cols],
-                in_=grouped[:, cols, :].rearrange("p n j -> p (n j)"),
+                out=codes.bitcast(FP8X4), scales=scales, in_=grouped.rearrange("p n j -> p (n j)")
             )
 
         def multiply(acc, e, s, codes, scales, cols):
@@ -93,56 +102,58 @@ def tile_moe_s_lin_silu_kernel(tc, x_words, x_scales, w, offs, out):
                 stop=(s == PASSES - 1),
             )
 
-        last = E - 1
-        half = N // 2
-        blocks = [slice(b * P, (b + 1) * P) for b in range(N // P)]
+
+        def stage(turn, width):
+            return keep.tile([P, width, PACK], BF16, name="staged", tag="stage%d" % (turn % 3), align_bytes=64)
+
+        def prepare(e, s, pieces):
+            turn = e * PASSES + s
+            if len(pieces) == 2:
+                staged = [stage(turn, half)[:], stage(turn + 1, half)[:]]
+            else:
+                high = stage(turn + 1, half)
+                staged = [stage(turn - 1, P)[:], high[:, :P], stage(turn, P)[:], high[:, P:]]
+            codes = keep.tile([P, N], U32, name="codes%d_%d" % (e, s), align_bytes=64)
+            scales = keep.tile([P, N], U8, name="scales%d_%d" % (e, s), align_bytes=64)
+            width = N // len(pieces)
+            for pair in range(0, len(pieces), 2):
+                group(nc.vector.tensor_copy, staged[pair], pieces[pair])
+                group(nc.scalar.copy, staged[pair + 1], pieces[pair + 1])
+                for i in (pair, pair + 1):
+                    cols = slice(i * width, (i + 1) * width)
+                    quantise(codes[:, cols], scales[:, cols], staged[i])
+            return codes, scales
+
         sums = []
         for e in range(last):
-            raw = keep.tile([P, PASSES, PACK, N], F32, name="raw", tag="slot%d" % (e % RAW_SLOTS))
-            step = PASSES if e < last - 1 else PASSES // 2
-            for s0 in range(0, PASSES, step):
-                load(raw, e, s0, s0 + step)
             acc = psum.tile([P, N], F32, name="acc", tag="bank%d" % e)
-            sums.append(acc)
             for s in range(PASSES):
-                grouped = stage.tile([P, N, PACK], BF16, name="grouped", align_bytes=64)
-                group(nc.scalar.copy, grouped, raw[:, s], slice(half, N))
-                group(nc.vector.tensor_copy, grouped, raw[:, s], slice(0, half))
-                codes = keep.tile([P, N], U32, name="codes%d_%d" % (e, s), align_bytes=64)
-                scales = keep.tile([P, N], U8, name="scales%d_%d" % (e, s), align_bytes=64)
-                quantise(codes, scales, grouped, slice(0, N))
+                codes, scales = prepare(e, s, load(e, s))
                 multiply(acc[:], e, s, codes, scales, slice(0, N))
+            sums.append(acc)
 
-        raw = keep.tile([P, PASSES, PACK, N], F32, name="raw", tag="slot%d" % (last % RAW_SLOTS))
-        for s in range(PASSES):
-            load(raw, last, s, s + 1)
+        blocks = [slice(b * P, (b + 1) * P) for b in range(N // P)]
+        loaded = [load(last, s) for s in range(PASSES - 1)]
+        halves = keep.tile([P, 2, PACK, half], F32, name="halves", tag=slot(last, PASSES - 1))
+        for h in range(2):
+            nc.sync.dma_start(out=halves[:, h], in_=rows_of(last, PASSES - 1)[:, :, h * half : (h + 1) * half])
+        loaded.append([halves[:, b // 2, :, (b % 2) * P : (b % 2 + 1) * P] for b in range(len(blocks))])
 
-        early = keep.tile([P, last - 1, N], F32, name="early", tag="slot%d" % ((last - 2) % RAW_SLOTS))
+        early = keep.tile([P, last - 1, N], F32, name="early", tag=slot(last - 1, 0))
         for e in range(last - 1):
             nc.scalar.activation(early[:, e, :], sums[e][:], SILU)
         nc.sync.dma_start(out=out[: (last - 1) * C, :].rearrange("(e p) n -> p e n", p=P), in_=early[:])
-        result = keep.tile([P, N], F32, name="result")
-        nc.scalar.activation(result[:], sums[last - 1][:], SILU)
-        nc.sync.dma_start(out=out[(last - 1) * C : last * C, :], in_=result[:])
+        result = keep.tile([P, N], F32, name="result", tag=slot(last, 0))
 
         accs = [psum.tile([P, P], F32, name="acc", tag="bank%d" % ((last + b) % 8)) for b in range(len(blocks))]
-        final = keep.tile([P, N], F32, name="final")
         for s in range(PASSES):
-            grouped = stage.tile([P, N, PACK], BF16, name="grouped", align_bytes=64)
-            codes = keep.tile([P, N], U32, name="codes%d_%d" % (last, s), align_bytes=64)
-            scales = keep.tile([P, N], U8, name="scales%d_%d" % (last, s), align_bytes=64)
-            if s < PASSES - 1:
-                group(nc.scalar.copy, grouped, raw[:, s], slice(half, N))
-                group(nc.vector.tensor_copy, grouped, raw[:, s], slice(0, half))
-                quantise(codes, scales, grouped, slice(0, N))
-                for b, cols in enumerate(blocks):
-                    multiply(accs[b][:], last, s, codes, scales, cols)
-            else:
-                for b, cols in enumerate(blocks):
-                    group(nc.vector.tensor_copy if b < 2 else nc.scalar.copy, grouped, raw[:, s], cols)
-                for b, cols in enumerate(blocks):
-                    quantise(codes, scales, grouped, cols)
-                    multiply(accs[b][:], last, s, codes, scales, cols)
+            codes, scales = prepare(last, s, loaded[s])
+            for b, cols in enumerate(blocks):
+                multiply(accs[b][:], last, s, codes, scales, cols)
+            if s == 0:
+                nc.scalar.activation(result[:], sums[last - 1][:], SILU)
+                nc.sync.dma_start(out=out[(last - 1) * C : last * C, :], in_=result[:])
+        final = keep.tile([P, N], F32, name="final", tag=slot(last, PASSES - 1))
         for b, cols in enumerate(blocks):
             nc.scalar.activation(final[:, cols], accs[b][:], SILU)
             if b % 2 == 1:

@@ -8,7 +8,10 @@ PACK = 4
 K_PASS = P * PACK
 PASSES = K // K_PASS
 SLOTS = E * C
-RAW_SLOTS = 10
+QUADRANT = 32
+BANKS = 8
+LANDINGS = 10
+STAGES = 3
 FLOPS = 2 * SLOTS * K * N
 
 F32 = mybir.dt.float32
@@ -29,9 +32,9 @@ def tile_moe_s_lin_silu_kernel(tc, x_words, x_scales, w, offs, out):
         psum = ctx.enter_context(tc.psum_pool(name="psum", bufs=1))
 
         scale_table = keep.tile([P, T], U8, name="scale_table", align_bytes=64)
-        planes = keep.tile([P, PASSES * SLOTS], U8, name="planes", align_bytes=64)
+        token_planes = keep.tile([P, PASSES * SLOTS], U8, name="token_planes", align_bytes=64)
         nc.vector.memset(scale_table[:].bitcast(I32), 0)
-        nc.vector.memset(planes[:].bitcast(I32), 0)
+        nc.vector.memset(token_planes[:].bitcast(I32), 0)
 
         offsets = keep.tile([P, SLOTS // 16], U16, name="offsets")
         word_tables = []
@@ -48,13 +51,13 @@ def tile_moe_s_lin_silu_kernel(tc, x_words, x_scales, w, offs, out):
 
         slot_scales = keep.tile([P, SLOTS], U8, name="slot_scales", align_bytes=64)
         nc.vector.tensor_copy(slot_scales[:], scale_table[:].indirect(offsets[:]))
-        for q in range(4):
+        for top in range(0, P, QUADRANT):
             nc.scalar.dma_start(
-                out=planes[32 * q : 32 * q + 4, :].bitcast(I32),
-                in_=slot_scales[32 * q : 32 * q + 32 : 2, :].bitcast(I32),
+                out=token_planes[top : top + 4, :].bitcast(I32),
+                in_=slot_scales[top : top + QUADRANT : 2, :].bitcast(I32),
             )
 
-        tokens = []
+        token_words = []
         for m in range(PASSES // 2):
             pairs = keep.tile([P, SLOTS], U32, name="pairs%d" % m, align_bytes=64)
             nc.vector.tensor_copy(pairs[:], word_tables[m][:].bitcast(U32).indirect(offsets[:]))
@@ -63,99 +66,100 @@ def tile_moe_s_lin_silu_kernel(tc, x_words, x_scales, w, offs, out):
                 out=parted[:].bitcast(U16).rearrange("p (q j) -> p q j", q=2),
                 in_=pairs[:].bitcast(U16).rearrange("p (j q) -> p q j", q=2),
             )
-            tokens.append(parted)
+            token_words.append(parted)
 
         last = E - 1
         half = N // 2
 
         def rows_of(e, s):
-            return w[e, s * K_PASS : (s + 1) * K_PASS, :].rearrange("(p j) n -> p j n", j=PACK)
+            return w[e, s * K_PASS : (s + 1) * K_PASS, :].rearrange("(p r) n -> p r n", r=PACK)
 
-        def slot(e, s):
-            return "slot%d" % ((e * PASSES + s) % RAW_SLOTS)
+        def landing(e, s):
+            return "landing%d" % ((e * PASSES + s) % LANDINGS)
 
         def load(e, s):
-            raw = keep.tile([P, PACK, N], F32, name="raw", tag=slot(e, s))
+            raw = keep.tile([P, PACK, N], F32, name="raw", tag=landing(e, s))
             nc.sync.dma_start(out=raw[:], in_=rows_of(e, s))
             return [raw[:, :, :half], raw[:, :, half:]]
 
-        def group(copy, grouped, rows):
+        def cast(copy, staged, rows):
             copy(
-                out=grouped.rearrange("p (c i) j -> p c j i", i=2),
-                in_=rows.rearrange("p j (c i) -> p c j i", i=2),
-            )
-
-        def quantise(codes, scales, grouped):
-            nc.vector.quantize_mx(
-                out=codes.bitcast(FP8X4), scales=scales, in_=grouped.rearrange("p n j -> p (n j)")
+                out=staged.rearrange("p (c i) r -> p c r i", i=2),
+                in_=rows.rearrange("p r (c i) -> p c r i", i=2),
             )
 
         def multiply(acc, e, s, codes, scales, cols):
             first = (s % 2) * SLOTS + e * C
             nc.tensor.matmul_mx(
                 out=acc,
-                lhsT=tokens[s // 2][:, 2 * first : 2 * (first + C)].bitcast(FP4X4),
-                lhsT_scale=planes[:, s * SLOTS + e * C : s * SLOTS + (e + 1) * C],
+                lhsT=token_words[s // 2][:, 2 * first : 2 * (first + C)].bitcast(FP4X4),
+                lhsT_scale=token_planes[:, s * SLOTS + e * C : s * SLOTS + (e + 1) * C],
                 rhs=codes[:, cols].bitcast(FP8X4),
                 rhs_scale=scales[:, cols],
                 start=(s == 0),
                 stop=(s == PASSES - 1),
             )
 
-
         def stage(turn, width):
-            return keep.tile([P, width, PACK], BF16, name="staged", tag="stage%d" % (turn % 3), align_bytes=64)
+            return keep.tile([P, width, PACK], BF16, name="staged", tag="stage%d" % (turn % STAGES), align_bytes=64)
 
-        def prepare(e, s, pieces):
+        def quantise_pass(e, s, pieces):
             turn = e * PASSES + s
             if len(pieces) == 2:
                 staged = [stage(turn, half)[:], stage(turn + 1, half)[:]]
             else:
-                high = stage(turn + 1, half)
-                staged = [stage(turn - 1, P)[:], high[:, :P], stage(turn, P)[:], high[:, P:]]
+                shared = stage(turn + 1, half)
+                staged = [stage(turn - 1, P)[:], shared[:, :P], stage(turn, P)[:], shared[:, P:]]
             codes = keep.tile([P, N], U32, name="codes%d_%d" % (e, s), align_bytes=64)
             scales = keep.tile([P, N], U8, name="scales%d_%d" % (e, s), align_bytes=64)
             width = N // len(pieces)
-            for pair in range(0, len(pieces), 2):
-                group(nc.vector.tensor_copy, staged[pair], pieces[pair])
-                group(nc.scalar.copy, staged[pair + 1], pieces[pair + 1])
-                for i in (pair, pair + 1):
+            for even in range(0, len(pieces), 2):
+                cast(nc.vector.tensor_copy, staged[even], pieces[even])
+                cast(nc.scalar.copy, staged[even + 1], pieces[even + 1])
+                for i in (even, even + 1):
                     cols = slice(i * width, (i + 1) * width)
-                    quantise(codes[:, cols], scales[:, cols], staged[i])
+                    nc.vector.quantize_mx(
+                        out=codes[:, cols].bitcast(FP8X4),
+                        scales=scales[:, cols],
+                        in_=staged[i].rearrange("p n r -> p (n r)"),
+                    )
             return codes, scales
 
         sums = []
         for e in range(last):
             acc = psum.tile([P, N], F32, name="acc", tag="bank%d" % e)
             for s in range(PASSES):
-                codes, scales = prepare(e, s, load(e, s))
+                codes, scales = quantise_pass(e, s, load(e, s))
                 multiply(acc[:], e, s, codes, scales, slice(0, N))
             sums.append(acc)
 
         blocks = [slice(b * P, (b + 1) * P) for b in range(N // P)]
         loaded = [load(last, s) for s in range(PASSES - 1)]
-        halves = keep.tile([P, 2, PACK, half], F32, name="halves", tag=slot(last, PASSES - 1))
+        halves = keep.tile([P, 2, PACK, half], F32, name="halves", tag=landing(last, PASSES - 1))
         for h in range(2):
             nc.sync.dma_start(out=halves[:, h], in_=rows_of(last, PASSES - 1)[:, :, h * half : (h + 1) * half])
         loaded.append([halves[:, b // 2, :, (b % 2) * P : (b % 2 + 1) * P] for b in range(len(blocks))])
 
-        early = keep.tile([P, last - 1, N], F32, name="early", tag=slot(last - 1, 0))
+        early = keep.tile([P, last - 1, N], F32, name="early", tag=landing(last - 1, 0))
         for e in range(last - 1):
             nc.scalar.activation(early[:, e, :], sums[e][:], SILU)
         nc.sync.dma_start(out=out[: (last - 1) * C, :].rearrange("(e p) n -> p e n", p=P), in_=early[:])
-        result = keep.tile([P, N], F32, name="result", tag=slot(last, 0))
+        fifth = keep.tile([P, N], F32, name="fifth", tag=landing(last, 0))
 
-        accs = [psum.tile([P, P], F32, name="acc", tag="bank%d" % ((last + b) % 8)) for b in range(len(blocks))]
+        block_sums = [
+            psum.tile([P, P], F32, name="acc", tag="bank%d" % ((last + b) % BANKS)) for b in range(len(blocks))
+        ]
         for s in range(PASSES):
-            codes, scales = prepare(last, s, loaded[s])
+            codes, scales = quantise_pass(last, s, loaded[s])
             for b, cols in enumerate(blocks):
-                multiply(accs[b][:], last, s, codes, scales, cols)
+                multiply(block_sums[b][:], last, s, codes, scales, cols)
             if s == 0:
-                nc.scalar.activation(result[:], sums[last - 1][:], SILU)
-                nc.sync.dma_start(out=out[(last - 1) * C : last * C, :], in_=result[:])
-        final = keep.tile([P, N], F32, name="final", tag=slot(last, PASSES - 1))
+                nc.scalar.activation(fifth[:], sums[last - 1][:], SILU)
+                nc.sync.dma_start(out=out[(last - 1) * C : last * C, :], in_=fifth[:])
+
+        final = keep.tile([P, N], F32, name="final", tag=landing(last, PASSES - 1))
         for b, cols in enumerate(blocks):
-            nc.scalar.activation(final[:, cols], accs[b][:], SILU)
+            nc.scalar.activation(final[:, cols], block_sums[b][:], SILU)
             if b % 2 == 1:
-                both = slice((b - 1) * P, (b + 1) * P)
-                nc.sync.dma_start(out=out[last * C :, both], in_=final[:, both])
+                done = slice((b - 1) * P, (b + 1) * P)
+                nc.sync.dma_start(out=out[last * C :, done], in_=final[:, done])

@@ -134,11 +134,8 @@ def tile_moe_s_lin_silu_kernel(tc, x_words, x_scales, w, offs, out):
             sums.append(acc)
 
         blocks = [slice(b * P, (b + 1) * P) for b in range(N // P)]
-        loaded = [load(last, s) for s in range(PASSES - 1)]
-        halves = keep.tile([P, 2, PACK, half], F32, name="halves", tag=landing(last, PASSES - 1))
-        for h in range(2):
-            nc.sync.dma_start(out=halves[:, h], in_=rows_of(last, PASSES - 1)[:, :, h * half : (h + 1) * half])
-        loaded.append([halves[:, b // 2, :, (b % 2) * P : (b % 2 + 1) * P] for b in range(len(blocks))])
+        loaded = [load(last, s) for s in range(PASSES)]
+        loaded[-1] = [loaded[-1][b // 2][:, :, (b % 2) * P : (b % 2 + 1) * P] for b in range(len(blocks))]
 
         early = keep.tile([P, last - 1, N], F32, name="early", tag=landing(last - 1, 0))
         for e in range(last - 1):

@@ -12,6 +12,7 @@ QUADRANT = 32
 BANKS = 8
 LANDINGS = 10
 STAGES = 3
+BURST = 256
 FLOPS = 2 * SLOTS * K * N
 
 F32 = mybir.dt.float32
@@ -31,15 +32,15 @@ def tile_moe_s_lin_silu_kernel(tc, x_words, x_scales, w, offs, out):
         keep = ctx.enter_context(tc.tile_pool(name="keep", bufs=1))
         psum = ctx.enter_context(tc.psum_pool(name="psum", bufs=1))
 
-        scale_table = keep.tile([P, T], U8, name="scale_table", align_bytes=64)
-        token_planes = keep.tile([P, PASSES * SLOTS], U8, name="token_planes", align_bytes=64)
+        scale_table = keep.tile([P, T], U8, name="scale_table", align_bytes=BURST)
+        token_planes = keep.tile([P, PASSES * SLOTS], U8, name="token_planes", align_bytes=BURST)
         nc.vector.memset(scale_table[:].bitcast(I32), 0)
         nc.vector.memset(token_planes[:].bitcast(I32), 0)
 
         offsets = keep.tile([P, SLOTS // 16], U16, name="offsets")
         word_tables = []
         for m in range(PASSES // 2):
-            table = keep.tile([P, T], I32, name="word_table%d" % m, align_bytes=64)
+            table = keep.tile([P, T], I32, name="word_table%d" % m, align_bytes=BURST)
             nc.sync.dma_start(out=table[:], in_=x_words[m].rearrange("p t d -> p (t d)").bitcast(I32))
             word_tables.append(table)
             if m == 0:
@@ -49,7 +50,7 @@ def tile_moe_s_lin_silu_kernel(tc, x_words, x_scales, w, offs, out):
                     in_=x_scales.bitcast(I32).rearrange("s b t -> b s t"),
                 )
 
-        slot_scales = keep.tile([P, SLOTS], U8, name="slot_scales", align_bytes=64)
+        slot_scales = keep.tile([P, SLOTS], U8, name="slot_scales", align_bytes=BURST)
         nc.vector.tensor_copy(slot_scales[:], scale_table[:].indirect(offsets[:]))
         for top in range(0, P, QUADRANT):
             nc.scalar.dma_start(
@@ -78,7 +79,7 @@ def tile_moe_s_lin_silu_kernel(tc, x_words, x_scales, w, offs, out):
             return "landing%d" % ((e * PASSES + s) % LANDINGS)
 
         def load(e, s):
-            raw = keep.tile([P, PACK, N], F32, name="raw", tag=landing(e, s))
+            raw = keep.tile([P, PACK, N], F32, name="raw", tag=landing(e, s), align_bytes=BURST)
             nc.sync.dma_start(out=raw[:], in_=rows_of(e, s))
             return [raw[:, :, :half], raw[:, :, half:]]
 
@@ -137,11 +138,11 @@ def tile_moe_s_lin_silu_kernel(tc, x_words, x_scales, w, offs, out):
         loaded = [load(last, s) for s in range(PASSES)]
         loaded[-1] = [loaded[-1][b // 2][:, :, (b % 2) * P : (b % 2 + 1) * P] for b in range(len(blocks))]
 
-        early = keep.tile([P, last - 1, N], F32, name="early", tag=landing(last - 1, 0))
+        early = keep.tile([P, last - 1, N], F32, name="early", tag=landing(last - 1, 0), align_bytes=BURST)
         for e in range(last - 1):
             nc.scalar.activation(early[:, e, :], sums[e][:], SILU)
         nc.sync.dma_start(out=out[: (last - 1) * C, :].rearrange("(e p) n -> p e n", p=P), in_=early[:])
-        fifth = keep.tile([P, N], F32, name="fifth", tag=landing(last, 0))
+        fifth = keep.tile([P, N], F32, name="fifth", tag=landing(last, 0), align_bytes=BURST)
 
         block_sums = [
             psum.tile([P, P], F32, name="acc", tag="bank%d" % ((last + b) % BANKS)) for b in range(len(blocks))
@@ -154,7 +155,7 @@ def tile_moe_s_lin_silu_kernel(tc, x_words, x_scales, w, offs, out):
                 nc.scalar.activation(fifth[:], sums[last - 1][:], SILU)
                 nc.sync.dma_start(out=out[(last - 1) * C : last * C, :], in_=fifth[:])
 
-        final = keep.tile([P, N], F32, name="final", tag=landing(last, PASSES - 1))
+        final = keep.tile([P, N], F32, name="final", tag=landing(last, PASSES - 1), align_bytes=BURST)
         for b, cols in enumerate(blocks):
             nc.scalar.activation(final[:, cols], block_sums[b][:], SILU)
             if b % 2 == 1:

@@ -114,16 +114,20 @@ def tile_moe_s_lin_silu_kernel(tc, x_words, x_scales, w, offs, out):
             codes = keep.tile([P, N], U32, name="codes%d_%d" % (e, s), align_bytes=64)
             scales = keep.tile([P, N], U8, name="scales%d_%d" % (e, s), align_bytes=64)
             width = N // len(pieces)
-            for even in range(0, len(pieces), 2):
-                cast(nc.vector.tensor_copy, staged[even], pieces[even])
-                cast(nc.scalar.copy, staged[even + 1], pieces[even + 1])
-                for i in (even, even + 1):
-                    cols = slice(i * width, (i + 1) * width)
-                    nc.vector.quantize_mx(
-                        out=codes[:, cols].bitcast(FP8X4),
-                        scales=scales[:, cols],
-                        in_=staged[i].rearrange("p n r -> p (n r)"),
-                    )
+            cast(nc.vector.tensor_copy, staged[0], pieces[0])
+            cast(nc.scalar.copy, staged[1], pieces[1])
+            if len(pieces) == 4:
+                cut = P // 2
+                cast(nc.vector.tensor_copy, staged[2], pieces[2])
+                cast(nc.vector.tensor_copy, staged[3][:, :cut], pieces[3][:, :, :cut])
+                cast(nc.scalar.copy, staged[3][:, cut:], pieces[3][:, :, cut:])
+            for i in range(len(pieces)):
+                cols = slice(i * width, (i + 1) * width)
+                nc.vector.quantize_mx(
+                    out=codes[:, cols].bitcast(FP8X4),
+                    scales=scales[:, cols],
+                    in_=staged[i].rearrange("p n r -> p (n r)"),
+                )
             return codes, scales
 
         sums = []

@@ -145,8 +145,7 @@ def tile_moe_s_lin_silu_kernel(tc, x_words, x_scales, w, offs, out):
         early = keep.tile([P, last - 1, N], F32, name="early", tag=landing(last - 1, 0), align_bytes=BURST)
         for e in range(last - 1):
             nc.scalar.activation(early[:, e, :], sums[e][:], SILU)
-        nc.sync.dma_start(out=out[: (last - 1) * C, :].rearrange("(e p) n -> p e n", p=P), in_=early[:])
-        fifth = keep.tile([P, N], F32, name="fifth", tag=landing(last, 0), align_bytes=BURST)
+        fifth = keep.tile([P, N], F32, name="fifth", tag=landing(last, 1), align_bytes=BURST)
 
         block_sums = [
             psum.tile([P, P], F32, name="acc", tag="bank%d" % ((last + b) % BANKS)) for b in range(len(blocks))
@@ -155,9 +154,10 @@ def tile_moe_s_lin_silu_kernel(tc, x_words, x_scales, w, offs, out):
             codes, scales = quantise_pass(last, s, loaded[s])
             for b, cols in enumerate(blocks):
                 multiply(block_sums[b][:], last, s, codes, scales, cols)
-            if s == 0:
+            if s == 1:
                 nc.scalar.activation(fifth[:], sums[last - 1][:], SILU)
                 nc.sync.dma_start(out=out[(last - 1) * C : last * C, :], in_=fifth[:])
+                nc.sync.dma_start(out=out[: (last - 1) * C, :].rearrange("(e p) n -> p e n", p=P), in_=early[:])
 
         final = keep.tile([P, N], F32, name="final", tag=landing(last, PASSES - 1), align_bytes=BURST)
         for b, cols in enumerate(blocks):

@@ -13,6 +13,7 @@ BANKS = 8
 LANDINGS = 10
 STAGES = 3
 BURST = 256
+EARLY = 192
 FLOPS = 2 * SLOTS * K * N
 
 F32 = mybir.dt.float32
@@ -70,18 +71,18 @@ def tile_moe_s_lin_silu_kernel(tc, x_words, x_scales, w, offs, out):
             token_words.append(parted)
 
         last = E - 1
-        half = N // 2
+        turns = E * PASSES
 
-        def rows_of(e, s):
-            return w[e, s * K_PASS : (s + 1) * K_PASS, :].rearrange("(p r) n -> p r n", r=PACK)
+        def landing(turn):
+            return "landing%d" % (turn % LANDINGS)
 
-        def landing(e, s):
-            return "landing%d" % ((e * PASSES + s) % LANDINGS)
-
-        def load(e, s):
-            raw = keep.tile([P, PACK, N], F32, name="raw", tag=landing(e, s), align_bytes=BURST)
-            nc.sync.dma_start(out=raw[:], in_=rows_of(e, s))
-            return [raw[:, :, :half], raw[:, :, half:]]
+        def load(turn, cuts):
+            e, s = divmod(turn, PASSES)
+            raw = keep.tile([P, PACK * N], F32, name="raw", tag=landing(turn), align_bytes=BURST)
+            rows = w[e, s * K_PASS : (s + 1) * K_PASS, :].rearrange("(p r) n -> p (r n)", r=PACK)
+            for a, b in cuts:
+                nc.sync.dma_start(out=raw[:, a:b], in_=rows[:, a:b])
+            return raw[:].rearrange("p (r n) -> p r n", r=PACK)
 
         def cast(copy, staged, rows):
             copy(
@@ -89,7 +90,28 @@ def tile_moe_s_lin_silu_kernel(tc, x_words, x_scales, w, offs, out):
                 in_=rows.rearrange("p r (c i) -> p c r i", i=2),
             )
 
-        def multiply(acc, e, s, codes, scales, cols):
+        def quantise(turn, raw, shares):
+            codes = keep.tile([P, N], U32, name="codes%d" % turn, align_bytes=64)
+            scales = keep.tile([P, N], U8, name="scales%d" % turn, align_bytes=64)
+            width = N // len(shares)
+            tiles = []
+            for i, casts in enumerate(shares):
+                tag = "stage%d" % (turn % STAGES) if len(shares) == 1 else "block%d_%d" % (turn, i)
+                staged = keep.tile([P, width, PACK], BF16, name="staged", tag=tag, align_bytes=64)
+                for copy, a, b in casts:
+                    cast(copy, staged[:, a - i * width : b - i * width, :], raw[:, :, a:b])
+                tiles.append(staged)
+            for i, staged in enumerate(tiles):
+                cols = slice(i * width, (i + 1) * width)
+                nc.vector.quantize_mx(
+                    out=codes[:, cols].bitcast(FP8X4),
+                    scales=scales[:, cols],
+                    in_=staged[:].rearrange("p n r -> p (n r)"),
+                )
+            return codes, scales
+
+        def multiply(acc, turn, codes, scales, cols):
+            e, s = divmod(turn, PASSES)
             first = (s % 2) * SLOTS + e * C
             nc.tensor.matmul_mx(
                 out=acc,
@@ -101,65 +123,56 @@ def tile_moe_s_lin_silu_kernel(tc, x_words, x_scales, w, offs, out):
                 stop=(s == PASSES - 1),
             )
 
-        def stage(turn, width):
-            return keep.tile([P, width, PACK], BF16, name="staged", tag="stage%d" % (turn % STAGES), align_bytes=64)
-
-        def quantise_pass(e, s, pieces):
-            turn = e * PASSES + s
-            if len(pieces) == 2:
-                staged = [stage(turn, half)[:], stage(turn + 1, half)[:]]
-            else:
-                shared = stage(turn + 1, half)
-                staged = [stage(turn - 1, P)[:], shared[:, :P], stage(turn, P)[:], shared[:, P:]]
-            codes = keep.tile([P, N], U32, name="codes%d_%d" % (e, s), align_bytes=64)
-            scales = keep.tile([P, N], U8, name="scales%d_%d" % (e, s), align_bytes=64)
-            width = N // len(pieces)
-            cast(nc.vector.tensor_copy, staged[0], pieces[0])
-            cast(nc.scalar.copy, staged[1], pieces[1])
-            if len(pieces) == 4:
-                cut = P // 2
-                cast(nc.vector.tensor_copy, staged[2], pieces[2])
-                cast(nc.vector.tensor_copy, staged[3][:, :cut], pieces[3][:, :, :cut])
-                cast(nc.scalar.copy, staged[3][:, cut:], pieces[3][:, :, cut:])
-            for i in range(len(pieces)):
-                cols = slice(i * width, (i + 1) * width)
-                nc.vector.quantize_mx(
-                    out=codes[:, cols].bitcast(FP8X4),
-                    scales=scales[:, cols],
-                    in_=staged[i].rearrange("p n r -> p (n r)"),
-                )
-            return codes, scales
-
+        whole = [(0, PACK * N)]
+        half = N // 2
+        vector, scalar = nc.vector.tensor_copy, nc.scalar.copy
+        even = [(vector, 0, half), (scalar, half, N)]
         sums = []
         for e in range(last):
             acc = psum.tile([P, N], F32, name="acc", tag="bank%d" % e)
-            for s in range(PASSES):
-                codes, scales = quantise_pass(e, s, load(e, s))
-                multiply(acc[:], e, s, codes, scales, slice(0, N))
+            for turn in range(e * PASSES, (e + 1) * PASSES):
+                codes, scales = quantise(turn, load(turn, whole), [even])
+                multiply(acc[:], turn, codes, scales, slice(0, N))
             sums.append(acc)
 
-        blocks = [slice(b * P, (b + 1) * P) for b in range(N // P)]
-        loaded = [load(last, s) for s in range(PASSES)]
-        loaded[-1] = [loaded[-1][b // 2][:, :, (b % 2) * P : (b % 2 + 1) * P] for b in range(len(blocks))]
+        step = (PACK - 1) * N + EARLY
+        loaded = [load(turn, whole) for turn in range(last * PASSES, turns - 1)]
+        loaded.append(load(turns - 1, [(0, step), (step, PACK * N)]))
 
-        early = keep.tile([P, last - 1, N], F32, name="early", tag=landing(last - 1, 0), align_bytes=BURST)
+        early = keep.tile([P, last - 1, N], F32, name="early", tag=landing((last - 1) * PASSES), align_bytes=BURST)
         for e in range(last - 1):
             nc.scalar.activation(early[:, e, :], sums[e][:], SILU)
-        fifth = keep.tile([P, N], F32, name="fifth", tag=landing(last, 1), align_bytes=BURST)
+        fifth = keep.tile([P, N], F32, name="fifth", tag=landing(last * PASSES + 1), align_bytes=BURST)
 
+        blocks = [slice(b * P, (b + 1) * P) for b in range(N // P)]
         block_sums = [
             psum.tile([P, P], F32, name="acc", tag="bank%d" % ((last + b) % BANKS)) for b in range(len(blocks))
         ]
         for s in range(PASSES):
-            codes, scales = quantise_pass(last, s, loaded[s])
+            turn = last * PASSES + s
+            if s < PASSES - 2:
+                codes, scales = quantise(turn, loaded[s], [even])
+            elif s == PASSES - 2:
+                codes, scales = quantise(turn, loaded[s], [even[:1], even[1:]])
+            else:
+                codes, scales = quantise(
+                    turn,
+                    loaded[s],
+                    [
+                        [(vector, 0, P)],
+                        [(scalar, P, EARLY), (vector, EARLY, 2 * P)],
+                        [(vector, 2 * P, 3 * P)],
+                        [(scalar, 3 * P, N)],
+                    ],
+                )
             for b, cols in enumerate(blocks):
-                multiply(block_sums[b][:], last, s, codes, scales, cols)
+                multiply(block_sums[b][:], turn, codes, scales, cols)
             if s == 1:
                 nc.scalar.activation(fifth[:], sums[last - 1][:], SILU)
                 nc.sync.dma_start(out=out[(last - 1) * C : last * C, :], in_=fifth[:])
                 nc.sync.dma_start(out=out[: (last - 1) * C, :].rearrange("(e p) n -> p e n", p=P), in_=early[:])
 
-        final = keep.tile([P, N], F32, name="final", tag=landing(last, PASSES - 1), align_bytes=BURST)
+        final = keep.tile([P, N], F32, name="final", tag=landing(turns - 1), align_bytes=BURST)
         for b, cols in enumerate(blocks):
             nc.scalar.activation(final[:, cols], block_sums[b][:], SILU)
             if b % 2 == 1:

@@ -13,6 +13,8 @@ BANKS = 8
 LANDINGS = 10
 STAGES = 3
 BURST = 256
+ALONE = 3
+FIRST, STEP = 11, 7
 EARLY = 192
 FLOPS = 2 * SLOTS * K * N
 
@@ -33,48 +35,11 @@ def tile_moe_s_lin_silu_kernel(tc, x_words, x_scales, w, offs, out):
         keep = ctx.enter_context(tc.tile_pool(name="keep", bufs=1))
         psum = ctx.enter_context(tc.psum_pool(name="psum", bufs=1))
 
-        scale_table = keep.tile([P, T], U8, name="scale_table", align_bytes=BURST)
-        token_planes = keep.tile([P, PASSES * SLOTS], U8, name="token_planes", align_bytes=BURST)
-        nc.vector.memset(scale_table[:].bitcast(I32), 0)
-        nc.vector.memset(token_planes[:].bitcast(I32), 0)
-
-        offsets = keep.tile([P, SLOTS // 16], U16, name="offsets")
-        word_tables = []
-        for m in range(PASSES // 2):
-            table = keep.tile([P, T], I32, name="word_table%d" % m, align_bytes=BURST)
-            nc.sync.dma_start(out=table[:], in_=x_words[m].rearrange("p t d -> p (t d)").bitcast(I32))
-            word_tables.append(table)
-            if m == 0:
-                nc.sync.dma_start(offsets[:], offs)
-                nc.sync.dma_start(
-                    out=scale_table[0:P:2, :].bitcast(I32),
-                    in_=x_scales.bitcast(I32).rearrange("s b t -> b s t"),
-                )
-
-        slot_scales = keep.tile([P, SLOTS], U8, name="slot_scales", align_bytes=BURST)
-        nc.vector.tensor_copy(slot_scales[:], scale_table[:].indirect(offsets[:]))
-        for top in range(0, P, QUADRANT):
-            nc.scalar.dma_start(
-                out=token_planes[top : top + 4, :].bitcast(I32),
-                in_=slot_scales[top : top + QUADRANT : 2, :].bitcast(I32),
-            )
-
-        token_words = []
-        for m in range(PASSES // 2):
-            pairs = keep.tile([P, SLOTS], U32, name="pairs%d" % m, align_bytes=64)
-            nc.vector.tensor_copy(pairs[:], word_tables[m][:].bitcast(U32).indirect(offsets[:]))
-            parted = keep.tile([P, 2 * 2 * SLOTS], U8, name="parted%d" % m, align_bytes=64)
-            nc.vector.tensor_copy(
-                out=parted[:].bitcast(U16).rearrange("p (q j) -> p q j", q=2),
-                in_=pairs[:].bitcast(U16).rearrange("p (j q) -> p q j", q=2),
-            )
-            token_words.append(parted)
-
         last = E - 1
         turns = E * PASSES
 
         def landing(turn):
-            return "landing%d" % (turn % LANDINGS)
+            return "planes" if turn == ALONE - 1 else "landing%d" % ((turn - (turn >= ALONE)) % LANDINGS)
 
         def load(turn, cuts):
             e, s = divmod(turn, PASSES)
@@ -83,6 +48,32 @@ def tile_moe_s_lin_silu_kernel(tc, x_words, x_scales, w, offs, out):
             for a, b in cuts:
                 nc.sync.dma_start(out=raw[:, a:b], in_=rows[:, a:b])
             return raw[:].rearrange("p (r n) -> p r n", r=PACK)
+
+        whole = [(0, PACK * N)]
+        opening = [load(0, whole)]
+
+        scale_table = keep.tile([P, PASSES * T], U8, name="scale_table", align_bytes=BURST)
+        nc.vector.memset(scale_table[:].bitcast(I32), 0)
+
+        offsets = keep.tile([P, SLOTS // 16], U16, name="offsets")
+        nc.sync.dma_start(offsets[:], offs)
+        nc.sync.dma_start(
+            out=scale_table[FIRST : FIRST + 16 * STEP : STEP, :].bitcast(I32).rearrange("b (s t) -> b s t", s=PASSES),
+            in_=x_scales.bitcast(I32).rearrange("s b t -> b s t"),
+        )
+        opening.append(load(1, whole))
+        word_tables = []
+        for m in range(PASSES // 2):
+            opening.append(load(2 + m, whole))
+            table = keep.tile([P, T], I32, name="word_table%d" % m, align_bytes=BURST)
+            nc.sync.dma_start(out=table[:], in_=x_words[m].rearrange("p t d -> p (t d)").bitcast(I32))
+            word_tables.append(table)
+
+        slot_scales = keep.tile([P, PASSES * SLOTS], U8, name="slot_scales", align_bytes=BURST)
+        for s in range(PASSES):
+            nc.vector.tensor_copy(
+                slot_scales[:, s * SLOTS : (s + 1) * SLOTS], scale_table[:, s * T : (s + 1) * T].indirect(offsets[:])
+            )
 
         def cast(copy, staged, rows):
             copy(
@@ -123,15 +114,39 @@ def tile_moe_s_lin_silu_kernel(tc, x_words, x_scales, w, offs, out):
                 stop=(s == PASSES - 1),
             )
 
-        whole = [(0, PACK * N)]
         half = N // 2
         vector, scalar = nc.vector.tensor_copy, nc.scalar.copy
         even = [(vector, 0, half), (scalar, half, N)]
+        ahead = [quantise(turn, opening[turn], [[(scalar, 0, N)]]) for turn in range(ALONE)]
+        token_planes = keep.tile([P, PASSES * SLOTS], U8, name="token_planes", tag="planes", align_bytes=BURST)
+        nc.vector.memset(token_planes[:].bitcast(I32), 0)
+        for r in range(4):
+            top = FIRST + STEP * r
+            nc.scalar.dma_start(
+                out=token_planes[r:P:QUADRANT, :].bitcast(I32),
+                in_=slot_scales[top : top + 12 * STEP + 1 : 4 * STEP, :].bitcast(I32),
+            )
+
+        token_words = []
+        for m in range(PASSES // 2):
+            pairs = keep.tile([P, SLOTS], U32, name="pairs%d" % m, align_bytes=64)
+            nc.vector.tensor_copy(pairs[:], word_tables[m][:].bitcast(U32).indirect(offsets[:]))
+            parted = keep.tile([P, 2 * 2 * SLOTS], U8, name="parted%d" % m, align_bytes=64)
+            nc.vector.tensor_copy(
+                out=parted[:].bitcast(U16).rearrange("p (q j) -> p q j", q=2),
+                in_=pairs[:].bitcast(U16).rearrange("p (j q) -> p q j", q=2),
+            )
+            token_words.append(parted)
+
         sums = []
         for e in range(last):
             acc = psum.tile([P, N], F32, name="acc", tag="bank%d" % e)
             for turn in range(e * PASSES, (e + 1) * PASSES):
-                codes, scales = quantise(turn, load(turn, whole), [even])
+                if turn < ALONE:
+                    codes, scales = ahead[turn]
+                else:
+                    raw = opening[turn] if turn < len(opening) else load(turn, whole)
+                    codes, scales = quantise(turn, raw, [even])
                 multiply(acc[:], turn, codes, scales, slice(0, N))
             sums.append(acc)
 

@@ -190,6 +190,6 @@ def tile_moe_s_lin_silu_kernel(tc, x_words, x_scales, w, offs, out):
         final = keep.tile([P, N], F32, name="final", tag=landing(turns - 1), align_bytes=BURST)
         for b, cols in enumerate(blocks):
             nc.scalar.activation(final[:, cols], block_sums[b][:], SILU)
-            if b % 2 == 1:
-                done = slice((b - 1) * P, (b + 1) * P)
+            if b > 0:
+                done = slice(0 if b == 1 else b * P, (b + 1) * P)
                 nc.sync.dma_start(out=out[last * C :, done], in_=final[:, done])

@@ -146,7 +146,7 @@ def tile_moe_s_lin_silu_kernel(tc, x_words, x_scales, w, offs, out):
                     codes, scales = ahead[turn]
                 else:
                     raw = opening[turn] if turn < len(opening) else load(turn, whole)
-                    codes, scales = quantise(turn, raw, [even])
+                    codes, scales = quantise(turn, raw, [[(vector, 0, N)] if turn == (last - 1) * PASSES + 1 else even])
                 multiply(acc[:], turn, codes, scales, slice(0, N))
             sums.append(acc)
 
@@ -168,7 +168,7 @@ def tile_moe_s_lin_silu_kernel(tc, x_words, x_scales, w, offs, out):
             if s < PASSES - 2:
                 codes, scales = quantise(turn, loaded[s], [even])
             elif s == PASSES - 2:
-                codes, scales = quantise(turn, loaded[s], [even[:1], even[1:]])
+                codes, scales = quantise(turn, loaded[s], [even[:1], [(vector, half, half + P // 2), (scalar, half + P // 2, N)]])
             else:
                 codes, scales = quantise(
                     turn,

@@ -101,7 +101,7 @@ def tile_moe_s_lin_silu_kernel(tc, x_words, x_scales, w, offs, out):
                 )
             return codes, scales
 
-        def multiply(acc, turn, codes, scales, cols):
+        def multiply(acc, turn, codes, scales, cols, opener=0):
             e, s = divmod(turn, PASSES)
             first = (s % 2) * SLOTS + e * C
             nc.tensor.matmul_mx(
@@ -110,7 +110,7 @@ def tile_moe_s_lin_silu_kernel(tc, x_words, x_scales, w, offs, out):
                 lhsT_scale=token_planes[:, s * SLOTS + e * C : s * SLOTS + (e + 1) * C],
                 rhs=codes[:, cols].bitcast(FP8X4),
                 rhs_scale=scales[:, cols],
-                start=(s == 0),
+                start=(s == opener),
                 stop=(s == PASSES - 1),
             )
 
@@ -163,6 +163,7 @@ def tile_moe_s_lin_silu_kernel(tc, x_words, x_scales, w, offs, out):
         block_sums = [
             psum.tile([P, P], F32, name="acc", tag="bank%d" % ((last + b) % BANKS)) for b in range(len(blocks))
         ]
+        waiting = []
         for s in range(PASSES):
             turn = last * PASSES + s
             if s < PASSES - 2:
@@ -180,8 +181,12 @@ def tile_moe_s_lin_silu_kernel(tc, x_words, x_scales, w, offs, out):
                         [(scalar, 3 * P, N)],
                     ],
                 )
-            for b, cols in enumerate(blocks):
-                multiply(block_sums[b][:], turn, codes, scales, cols)
+            waiting = [(turn, codes, scales)] + waiting
+            if s >= PASSES - 2:
+                for b, cols in enumerate(blocks):
+                    for ready in waiting:
+                        multiply(block_sums[b][:], *ready, cols, opener=PASSES - 2)
+                waiting = []
             if s == 1:
                 nc.scalar.activation(fifth[:], sums[last - 1][:], SILU)
                 nc.sync.dma_start(out=out[(last - 1) * C : last * C, :], in_=fifth[:])

@@ -163,38 +163,49 @@ def tile_moe_s_lin_silu_kernel(tc, x_words, x_scales, w, offs, out):
         block_sums = [
             psum.tile([P, P], F32, name="acc", tag="bank%d" % ((last + b) % BANKS)) for b in range(len(blocks))
         ]
+        opener = PASSES - 2
         waiting = []
-        for s in range(PASSES):
+        for s in range(PASSES - 1):
             turn = last * PASSES + s
-            if s < PASSES - 2:
+            if s < opener:
                 codes, scales = quantise(turn, loaded[s], [even])
-            elif s == PASSES - 2:
-                codes, scales = quantise(turn, loaded[s], [even[:1], [(vector, half, half + P // 2), (scalar, half + P // 2, N)]])
             else:
-                codes, scales = quantise(
-                    turn,
-                    loaded[s],
-                    [
-                        [(vector, 0, P)],
-                        [(scalar, P, EARLY), (vector, EARLY, 2 * P)],
-                        [(vector, 2 * P, 3 * P)],
-                        [(scalar, 3 * P, N)],
-                    ],
-                )
+                cut = half + P // 2
+                codes, scales = quantise(turn, loaded[s], [even[:1], [(vector, half, cut), (scalar, cut, N)]])
             waiting = [(turn, codes, scales)] + waiting
-            if s >= PASSES - 2:
-                for b, cols in enumerate(blocks):
-                    for ready in waiting:
-                        multiply(block_sums[b][:], *ready, cols, opener=PASSES - 2)
-                waiting = []
             if s == 1:
                 nc.scalar.activation(fifth[:], sums[last - 1][:], SILU)
                 nc.sync.dma_start(out=out[(last - 1) * C : last * C, :], in_=fifth[:])
                 nc.sync.dma_start(out=out[: (last - 1) * C, :].rearrange("(e p) n -> p e n", p=P), in_=early[:])
+        order = [1, 0, 2, 3]
+        for b in order:
+            for ready in waiting:
+                multiply(block_sums[b][:], *ready, blocks[b], opener=opener)
+
+        shares = [
+            [(vector, 0, P)],
+            [(scalar, P, EARLY), (vector, EARLY, 2 * P)],
+            [(vector, 2 * P, 3 * P)],
+            [(scalar, 3 * P, N)],
+        ]
+        staged = []
+        for b, casts in enumerate(shares):
+            piece = keep.tile([P, P, PACK], BF16, name="piece", tag="piece%d" % b, align_bytes=64)
+            for copy, first, end in casts:
+                cast(copy, piece[:, first - b * P : end - b * P, :], loaded[-1][:, :, first:end])
+            staged.append(piece)
+        for b in order:
+            tag = "piece1" if b == 0 else "piece_codes%d" % b
+            codes = keep.tile([P, P], U32, name="codes", tag=tag, align_bytes=64)
+            scales = keep.tile([P, P], U8, name="piece_scales%d" % b, align_bytes=64)
+            nc.vector.quantize_mx(
+                out=codes[:].bitcast(FP8X4), scales=scales[:], in_=staged[b][:].rearrange("p n r -> p (n r)")
+            )
+            multiply(block_sums[b][:], turns - 1, codes, scales, slice(0, P), opener=opener)
 
         final = keep.tile([P, N], F32, name="final", tag=landing(turns - 1), align_bytes=BURST)
-        for b, cols in enumerate(blocks):
-            nc.scalar.activation(final[:, cols], block_sums[b][:], SILU)
-            if b > 0:
-                done = slice(0 if b == 1 else b * P, (b + 1) * P)
+        for b in order:
+            nc.scalar.activation(final[:, blocks[b]], block_sums[b][:], SILU)
+            if b != 1:
+                done = slice(blocks[b].start, max(half, blocks[b].stop))
                 nc.sync.dma_start(out=out[last * C :, done], in_=final[:, done])

@@ -163,24 +163,24 @@ def tile_moe_s_lin_silu_kernel(tc, x_words, x_scales, w, offs, out):
         block_sums = [
             psum.tile([P, P], F32, name="acc", tag="bank%d" % ((last + b) % BANKS)) for b in range(len(blocks))
         ]
-        opener = PASSES - 2
+        opener = 1
         waiting = []
         for s in range(PASSES - 1):
             turn = last * PASSES + s
-            if s < opener:
+            if s < PASSES - 2:
                 codes, scales = quantise(turn, loaded[s], [even])
             else:
                 cut = half + P // 2
                 codes, scales = quantise(turn, loaded[s], [even[:1], [(vector, half, cut), (scalar, cut, N)]])
-            waiting = [(turn, codes, scales)] + waiting
+            waiting.append((turn, codes, scales))
             if s == 1:
                 nc.scalar.activation(fifth[:], sums[last - 1][:], SILU)
                 nc.sync.dma_start(out=out[(last - 1) * C : last * C, :], in_=fifth[:])
                 nc.sync.dma_start(out=out[: (last - 1) * C, :].rearrange("(e p) n -> p e n", p=P), in_=early[:])
         order = [1, 0, 2, 3]
-        for b in order:
-            for ready in waiting:
-                multiply(block_sums[b][:], *ready, blocks[b], opener=opener)
+        for s in (1, 0, 2):
+            for b in order:
+                multiply(block_sums[b][:], *waiting[s], blocks[b], opener=opener)
 
         shares = [
             [(vector, 0, P)],

from contextlib import ExitStack

import concourse.mybir as mybir

K, T, E, C, N = 2048, 2048, 6, 128, 512
P = 128
PACK = 4
K_PASS = P * PACK
PASSES = K // K_PASS
SLOTS = E * C
QUADRANT = 32
BANKS = 8
LANDINGS = 10
STAGES = 3
BURST = 256
ALONE = 3
FIRST, STEP = 11, 7
EARLY = 192
FLOPS = 2 * SLOTS * K * N

F32 = mybir.dt.float32
BF16 = mybir.dt.bfloat16
I32 = mybir.dt.int32
U32 = mybir.dt.uint32
U16 = mybir.dt.uint16
U8 = mybir.dt.uint8
FP8X4 = mybir.dt.float8_e4m3fn_x4
FP4X4 = mybir.dt.float4_e2m1fn_x4
SILU = mybir.ActivationFunctionType.Silu


def tile_moe_s_lin_silu_kernel(tc, x_words, x_scales, w, offs, out):
    nc = tc.nc
    with ExitStack() as ctx:
        keep = ctx.enter_context(tc.tile_pool(name="keep", bufs=1))
        psum = ctx.enter_context(tc.psum_pool(name="psum", bufs=1))

        last = E - 1
        turns = E * PASSES

        def landing(turn):
            return "planes" if turn == ALONE - 1 else "landing%d" % ((turn - (turn >= ALONE)) % LANDINGS)

        def load(turn, cuts):
            e, s = divmod(turn, PASSES)
            raw = keep.tile([P, PACK * N], F32, name="raw", tag=landing(turn), align_bytes=BURST)
            rows = w[e, s * K_PASS : (s + 1) * K_PASS, :].rearrange("(p r) n -> p (r n)", r=PACK)
            for a, b in cuts:
                nc.sync.dma_start(out=raw[:, a:b], in_=rows[:, a:b])
            return raw[:].rearrange("p (r n) -> p r n", r=PACK)

        whole = [(0, PACK * N)]
        opening = [load(0, whole)]

        scale_table = keep.tile([P, PASSES * T], U8, name="scale_table", align_bytes=BURST)
        nc.vector.memset(scale_table[:].bitcast(I32), 0)

        offsets = keep.tile([P, SLOTS // 16], U16, name="offsets")
        nc.sync.dma_start(offsets[:], offs)
        nc.sync.dma_start(
            out=scale_table[FIRST : FIRST + 16 * STEP : STEP, :].bitcast(I32).rearrange("b (s t) -> b s t", s=PASSES),
            in_=x_scales.bitcast(I32).rearrange("s b t -> b s t"),
        )
        opening.append(load(1, whole))
        word_tables = []
        for m in range(PASSES // 2):
            opening.append(load(2 + m, whole))
            table = keep.tile([P, T], I32, name="word_table%d" % m, align_bytes=BURST)
            nc.sync.dma_start(out=table[:], in_=x_words[m].rearrange("p t d -> p (t d)").bitcast(I32))
            word_tables.append(table)

        slot_scales = keep.tile([P, PASSES * SLOTS], U8, name="slot_scales", align_bytes=BURST)
        for s in range(PASSES):
            nc.vector.tensor_copy(
                slot_scales[:, s * SLOTS : (s + 1) * SLOTS], scale_table[:, s * T : (s + 1) * T].indirect(offsets[:])
            )

        def cast(copy, staged, rows):
            copy(
                out=staged.rearrange("p (c i) r -> p c r i", i=2),
                in_=rows.rearrange("p r (c i) -> p c r i", i=2),
            )

        def quantise(turn, raw, shares):
            codes = keep.tile([P, N], U32, name="codes%d" % turn, align_bytes=64)
            scales = keep.tile([P, N], U8, name="scales%d" % turn, align_bytes=64)
            width = N // len(shares)
            tiles = []
            for i, casts in enumerate(shares):
                tag = "stage%d" % (turn % STAGES) if len(shares) == 1 else "block%d_%d" % (turn, i)
                staged = keep.tile([P, width, PACK], BF16, name="staged", tag=tag, align_bytes=64)
                for copy, a, b in casts:
                    cast(copy, staged[:, a - i * width : b - i * width, :], raw[:, :, a:b])
                tiles.append(staged)
            for i, staged in enumerate(tiles):
                cols = slice(i * width, (i + 1) * width)
                nc.vector.quantize_mx(
                    out=codes[:, cols].bitcast(FP8X4),
                    scales=scales[:, cols],
                    in_=staged[:].rearrange("p n r -> p (n r)"),
                )
            return codes, scales

        def multiply(acc, turn, codes, scales, cols, opener=0):
            e, s = divmod(turn, PASSES)
            first = (s % 2) * SLOTS + e * C
            nc.tensor.matmul_mx(
                out=acc,
                lhsT=token_words[s // 2][:, 2 * first : 2 * (first + C)].bitcast(FP4X4),
                lhsT_scale=token_planes[:, s * SLOTS + e * C : s * SLOTS + (e + 1) * C],
                rhs=codes[:, cols].bitcast(FP8X4),
                rhs_scale=scales[:, cols],
                start=(s == opener),
                stop=(s == PASSES - 1),
            )

        half = N // 2
        vector, scalar = nc.vector.tensor_copy, nc.scalar.copy
        even = [(vector, 0, half), (scalar, half, N)]
        ahead = [quantise(turn, opening[turn], [[(scalar, 0, N)]]) for turn in range(ALONE)]
        token_planes = keep.tile([P, PASSES * SLOTS], U8, name="token_planes", tag="planes", align_bytes=BURST)
        nc.vector.memset(token_planes[:].bitcast(I32), 0)
        for r in range(4):
            top = FIRST + STEP * r
            nc.scalar.dma_start(
                out=token_planes[r:P:QUADRANT, :].bitcast(I32),
                in_=slot_scales[top : top + 12 * STEP + 1 : 4 * STEP, :].bitcast(I32),
            )

        token_words = []
        for m in range(PASSES // 2):
            pairs = keep.tile([P, SLOTS], U32, name="pairs%d" % m, align_bytes=64)
            nc.vector.tensor_copy(pairs[:], word_tables[m][:].bitcast(U32).indirect(offsets[:]))
            parted = keep.tile([P, 2 * 2 * SLOTS], U8, name="parted%d" % m, align_bytes=64)
            nc.vector.tensor_copy(
                out=parted[:].bitcast(U16).rearrange("p (q j) -> p q j", q=2),
                in_=pairs[:].bitcast(U16).rearrange("p (j q) -> p q j", q=2),
            )
            token_words.append(parted)

        sums = []
        for e in range(last):
            acc = psum.tile([P, N], F32, name="acc", tag="bank%d" % e)
            for turn in range(e * PASSES, (e + 1) * PASSES):
                if turn < ALONE:
                    codes, scales = ahead[turn]
                else:
                    raw = opening[turn] if turn < len(opening) else load(turn, whole)
                    codes, scales = quantise(turn, raw, [[(vector, 0, N)] if turn == (last - 1) * PASSES + 1 else even])
                multiply(acc[:], turn, codes, scales, slice(0, N))
            sums.append(acc)

        step = (PACK - 1) * N + EARLY
        loaded = [load(turn, whole) for turn in range(last * PASSES, turns - 1)]
        loaded.append(load(turns - 1, [(0, step), (step, PACK * N)]))

        early = keep.tile([P, last - 1, N], F32, name="early", tag=landing((last - 1) * PASSES), align_bytes=BURST)
        for e in range(last - 1):
            nc.scalar.activation(early[:, e, :], sums[e][:], SILU)
        fifth = keep.tile([P, N], F32, name="fifth", tag=landing(last * PASSES + 1), align_bytes=BURST)

        blocks = [slice(b * P, (b + 1) * P) for b in range(N // P)]
        block_sums = [
            psum.tile([P, P], F32, name="acc", tag="bank%d" % ((last + b) % BANKS)) for b in range(len(blocks))
        ]
        opener = 1
        waiting = []
        for s in range(PASSES - 1):
            turn = last * PASSES + s
            if s < PASSES - 2:
                codes, scales = quantise(turn, loaded[s], [even])
            else:
                cut = half + P // 2
                codes, scales = quantise(turn, loaded[s], [even[:1], [(vector, half, cut), (scalar, cut, N)]])
            waiting.append((turn, codes, scales))
            if s == 1:
                nc.scalar.activation(fifth[:], sums[last - 1][:], SILU)
                nc.sync.dma_start(out=out[(last - 1) * C : last * C, :], in_=fifth[:])
                nc.sync.dma_start(out=out[: (last - 1) * C, :].rearrange("(e p) n -> p e n", p=P), in_=early[:])
        order = [1, 0, 2, 3]
        for s in (1, 0, 2):
            for b in order:
                multiply(block_sums[b][:], *waiting[s], blocks[b], opener=opener)

        shares = [
            [(vector, 0, P)],
            [(scalar, P, EARLY), (vector, EARLY, 2 * P)],
            [(vector, 2 * P, 3 * P)],
            [(scalar, 3 * P, N)],
        ]
        staged = []
        for b, casts in enumerate(shares):
            piece = keep.tile([P, P, PACK], BF16, name="piece", tag="piece%d" % b, align_bytes=64)
            for copy, first, end in casts:
                cast(copy, piece[:, first - b * P : end - b * P, :], loaded[-1][:, :, first:end])
            staged.append(piece)
        for b in order:
            tag = "piece1" if b == 0 else "piece_codes%d" % b
            codes = keep.tile([P, P], U32, name="codes", tag=tag, align_bytes=64)
            scales = keep.tile([P, P], U8, name="piece_scales%d" % b, align_bytes=64)
            nc.vector.quantize_mx(
                out=codes[:].bitcast(FP8X4), scales=scales[:], in_=staged[b][:].rearrange("p n r -> p (n r)")
            )
            multiply(block_sums[b][:], turns - 1, codes, scales, slice(0, P), opener=opener)

        final = keep.tile([P, N], F32, name="final", tag=landing(turns - 1), align_bytes=BURST)
        for b in order:
            nc.scalar.activation(final[:, blocks[b]], block_sums[b][:], SILU)
            if b != 1:
                done = slice(blocks[b].start, max(half, blocks[b].stop))
                nc.sync.dma_start(out=out[last * C :, done], in_=final[:, done])
